import numpy as np
import ml_dtypes


def mxq(x, axis, fmt="e4m3"):
    dtype, down = {"e4m3": (ml_dtypes.float8_e4m3fn, 7), "e5m2": (ml_dtypes.float8_e5m2, 14)}[fmt]
    v = np.moveaxis(np.asarray(x, np.float32).astype(ml_dtypes.bfloat16).astype(np.float64), axis, -1)
    blocks = v.reshape(v.shape[:-1] + (-1, 32))
    amax = np.abs(blocks).max(-1, keepdims=True)
    byte = np.maximum(np.where(amax > 0, np.frexp(amax)[1] - 1 + 127, 0) - down, 1)
    scale = np.exp2(byte - 127.0)
    codes = (blocks / scale).astype(np.float32).astype(dtype).astype(np.float64)
    return np.moveaxis((codes * scale).reshape(v.shape), -1, axis)


WIDE = False


def mx_kscale(k):
    if not WIDE:
        return np.ones(k)
    levels = np.array([30, -30])
    if k % 512:
        return np.exp2(np.random.permutation(np.resize(levels, k // 32))).repeat(32)
    a = np.empty((k // 512, 16))
    for p in range(k // 512):
        a[p, :8] = np.random.permutation(np.resize(levels, 8))
        for g in range(8):
            far = levels[np.abs(levels - a[p, g]) >= 10]
            a[p, g + 8] = far[np.random.randint(len(far))]
    return np.exp2(a.ravel()).repeat(32)


def f64(x):
    return np.asarray(x).astype(np.float64)


def striped(idx):
    return np.tile(np.asarray(idx).reshape(-1, 16).T, (8, 1)).astype(np.uint16)


def unstriped(offs):
    return offs[:16].T.reshape(-1).astype(np.int64)


E2M1 = np.array([0.0, 0.5, 1.0, 1.5, 2.0, 3.0, 4.0, 6.0, -0.0, -0.5, -1.0, -1.5, -2.0, -3.0, -4.0, -6.0])


def pack_weight(w, fmt):
    k, n = w.shape
    w = f64(np.asarray(w, np.float32).astype(ml_dtypes.bfloat16)).reshape(k // 32, 32, n)
    amax = np.abs(w).max(1)
    if fmt in ("e4m3", "e5m2"):
        byte = np.frexp(amax)[1] - 1 + 127 - (7 if fmt == "e4m3" else 14)
    else:
        mant, ex = np.frexp(amax / 6.0)
        byte = np.where(mant > 0.5, ex, ex - 1) + 127
    byte = np.clip(np.where(amax > 0, byte, 1), 1, 254)
    scaled = (w * np.exp2(127.0 - byte)[:, None, :]).reshape(k, n).astype(np.float32)
    by_word = np.ascontiguousarray(scaled.reshape(k // 512, 128, 4, n).transpose(0, 1, 3, 2))
    if fmt in ("e4m3", "e5m2"):
        words = by_word.astype(ml_dtypes.float8_e4m3fn if fmt == "e4m3" else ml_dtypes.float8_e5m2).view(np.uint8)
    else:
        c = by_word.astype(ml_dtypes.float4_e2m1fn).view(np.uint8) & 0xF
        words = (c[..., 0::2] | (c[..., 1::2] << 4)).reshape(k // 512, 128, 2 * n)
    return np.ascontiguousarray(words), np.ascontiguousarray(byte.astype(np.uint8).reshape(k // 512, 16, n))


def unpack_weight(words, scales, fmt):
    g, _, n = scales.shape
    words = np.ascontiguousarray(words).reshape(g, 128, n, -1)
    if fmt in ("e4m3", "e5m2"):
        vals = words.view(ml_dtypes.float8_e4m3fn if fmt == "e4m3" else ml_dtypes.float8_e5m2).astype(np.float64)
    else:
        nib = np.empty((g, 128, n, 4), np.uint8)
        nib[..., 0::2] = words & 0xF
        nib[..., 1::2] = words >> 4
        vals = E2M1[nib]
    vals = vals * np.repeat(np.exp2(scales.astype(np.float64) - 127.0), 8, axis=1)[..., None]
    return vals.transpose(0, 1, 3, 2).reshape(g * 512, n)


K, T, J, R, N, C, O = 512, 1024, 256, 512, 256, 512, 128


def setup_inputs():
    n = np.random.standard_normal
    idx = np.random.permutation(T)[:J]
    idx2 = np.random.permutation(C)[:J]
    idx3 = np.random.permutation(C)[:O]
    idx4 = np.random.permutation(J)[:O]
    fk = mx_kscale(K)
    fr = mx_kscale(R)
    xtp = pack_weight(n((K, T)) / fk[:, None], "e5m2")
    wp = pack_weight(n((K, R)) * 1 / np.sqrt(K) * fk[:, None] * fr, "e2m1")
    w2p = pack_weight(n((K, R)) * 1 / np.sqrt(K) * fk[:, None] * fr, "e4m3")
    wbp = pack_weight(n((R, N)) * 1 / np.sqrt(R) / fr[:, None], "e2m1")
    wcp = pack_weight(n((R, N)) * 1 / np.sqrt(R) / fr[:, None], "e4m3")
    return {
        "xt_words": xtp[0],
        "xt_scales": xtp[1],
        "w_words": wp[0],
        "w_scales": wp[1],
        "w2_words": w2p[0],
        "w2_scales": w2p[1],
        "wb_words": wbp[0],
        "wb_scales": wbp[1],
        "wc_words": wcp[0],
        "wc_scales": wcp[1],
        "so": (np.random.uniform(0.5, 1.6, (N, 1))).astype(np.float32),
        "offs": striped(idx),
        "offs2": striped(idx2),
        "offs3": striped(idx3),
        "offs4": striped(idx4),
    }


def reference(xt_words, xt_scales, w_words, w_scales, w2_words, w2_scales, wb_words, wb_scales, wc_words, wc_scales, so, offs, offs2, offs3, offs4):
    idx = unstriped(offs)
    idx2 = unstriped(offs2)
    idx3 = unstriped(offs3)
    idx4 = unstriped(offs4)
    xtu = unpack_weight(xt_words, xt_scales, "e5m2")
    wu = unpack_weight(w_words, w_scales, "e2m1")
    w2u = unpack_weight(w2_words, w2_scales, "e4m3")
    wbu = unpack_weight(wb_words, wb_scales, "e2m1")
    wcu = unpack_weight(wc_words, wc_scales, "e4m3")
    xtidxg = xtu[:, idx]
    a = wu.T @ xtidxg
    b = w2u.T @ xtidxg
    hid = np.maximum(a, b)
    hidq = mxq(hid, 0, "e4m3")
    p = wbu.T @ hidq
    q = wcu.T @ hidq
    pw = np.zeros((N, C))
    pw[:, idx2] = p
    y = np.abs(pw[:, idx3] * f64(so) - q[:, idx4])
    return y

@@ -1,0 +1,182 @@
+from contextlib import ExitStack
+
+import concourse.mybir as mybir
+
+K, T, J, R, N, C, O = 512, 1024, 256, 512, 256, 512, 128
+FLOPS = 2 * 2 * K * R * J + 2 * 2 * R * N * J
+
+F32 = mybir.dt.float32
+BF16 = mybir.dt.bfloat16
+I32 = mybir.dt.int32
+U32 = mybir.dt.uint32
+U16 = mybir.dt.uint16
+U8 = mybir.dt.uint8
+E4M3 = mybir.dt.float8_e4m3fn_x4
+E5M2 = mybir.dt.float8_e5m2_x4
+E2M1 = mybir.dt.float4_e2m1fn_x4
+ALU = mybir.AluOpType
+COPY = mybir.ActivationFunctionType.Copy
+
+P = 128
+PACK = 4
+QUADS = 4
+QUAD = 32
+HALF = J // 2
+HALVES = 2
+NT = N // P
+
+
+def tile_list_outcomeboard_twow_kernel(
+    tc, xt_words, xt_scales, w_words, w_scales, w2_words, w2_scales, wb_words, wb_scales,
+    wc_words, wc_scales, so, offs, offs2, offs3, offs4, out,
+):
+    nc = tc.nc
+    with ExitStack() as ctx:
+        sb = ctx.enter_context(tc.tile_pool(name="sb", bufs=1))
+        ps = ctx.enter_context(tc.psum_pool(name="ps", bufs=1))
+
+        def staged_rows(scales):
+            return scales[0].bitcast(I32).rearrange("(q r) c -> r q c", r=PACK)
+
+        def flat_words(words):
+            return words[0].rearrange("p c t -> p (c t)").bitcast(I32)
+
+        list1 = sb.tile([P, J // 16], U16, name="list1")
+        list2 = sb.tile([P, J // 16], U16, name="list2")
+        list3 = sb.tile([P, O // 16], U16, name="list3")
+        list4 = sb.tile([P, O // 16], U16, name="list4")
+        x_words = sb.tile([P, T], U32, name="x_words", align_bytes=64)
+        x_plane = sb.tile([P, T], U8, name="x_plane", align_bytes=64)
+        w2_raw = sb.tile([P, R], U32, name="w2_raw", align_bytes=64)
+        w_raw = sb.tile([P, R], U16, name="w_raw", align_bytes=64)
+        s1_raw = sb.tile([P, QUADS, 2 * R], U8, name="s1_raw", align_bytes=64)
+        w2_plane = sb.tile([P, R], U8, name="w2_plane", align_bytes=64)
+        w_plane = sb.tile([P, R], U8, name="w_plane", align_bytes=64)
+        w2_dealt = sb.tile([P, R], U32, name="w2_dealt", align_bytes=64)
+        w_dealt = sb.tile([P, R], U16, name="w_dealt", align_bytes=64)
+        wb_sb = sb.tile([P, 2 * N], U8, name="wb_sb", align_bytes=64)
+        wc_sb = sb.tile([P, N], U32, name="wc_sb", align_bytes=64)
+        s2_raw = sb.tile([P, QUADS, 2 * N], U8, name="s2_raw", align_bytes=64)
+        s2_plane = s2_raw[:, 0, :]
+        so_sb = sb.tile([P, NT], F32, name="so_sb")
+        boards = [sb.tile([P, C], F32, name=f"board{i}") for i in range(NT)]
+
+        nc.vector.memset(s1_raw[:, 0, :].bitcast(I32), 0)
+        nc.vector.memset(x_plane[:].bitcast(I32), 0)
+        nc.vector.memset(s2_plane.bitcast(I32), 0)
+        nc.scalar.dma_start(x_words[:].bitcast(I32), flat_words(xt_words))
+        nc.gpsimd.dma_start(w2_raw[:].bitcast(I32), flat_words(w2_words))
+        nc.gpsimd.dma_start(w_raw[:].bitcast(I32), w_words[0].bitcast(I32))
+        nc.sync.dma_start(list1[:], offs)
+        nc.sync.dma_start(s1_raw[0:PACK, :, 0:R].bitcast(I32), staged_rows(w2_scales))
+        nc.sync.dma_start(s1_raw[0:PACK, :, R : 2 * R].bitcast(I32), staged_rows(w_scales))
+        for q in range(QUADS):
+            nc.sync.dma_start(
+                x_plane[QUAD * q : QUAD * q + PACK, :].bitcast(I32), xt_scales[0, PACK * q : PACK * (q + 1), :].bitcast(I32)
+            )
+        nc.sync.dma_start(s2_raw[0:PACK, :, 0:N].bitcast(I32), staged_rows(wb_scales))
+        nc.sync.dma_start(s2_raw[0:PACK, :, N : 2 * N].bitcast(I32), staged_rows(wc_scales))
+        nc.sync.dma_start(wb_sb[:].bitcast(I32), wb_words[0].bitcast(I32))
+        nc.sync.dma_start(wc_sb[:].bitcast(I32), flat_words(wc_words))
+        nc.sync.dma_start(list2[:], offs2)
+        nc.sync.dma_start(list4[:], offs4)
+        nc.sync.dma_start(list3[:], offs3)
+        with nc.allow_non_contiguous_dma(reason="one weight a partition"):
+            nc.sync.dma_start(so_sb[:], so.rearrange("(i p) one -> p (i one)", p=P))
+        for board in boards:
+            nc.vector.memset(board[:], 0.0)
+
+        def spread(raw):
+            for q in range(1, QUADS):
+                nc.vector.tensor_copy(raw[QUAD * q : QUAD * q + PACK, 0, :].bitcast(I32), raw[0:PACK, q, :].bitcast(I32))
+
+        def dealt(ap):
+            return ap.rearrange("p (t m) -> p t m", t=PACK)
+
+        def natural(ap):
+            return ap.rearrange("p (m t) -> p t m", t=PACK)
+
+        g_words = [sb.tile([P, HALF], U32, name=f"g_words{h}", align_bytes=64) for h in range(HALVES)]
+        g_plane = [sb.tile([P, HALF], U8, name=f"g_plane{h}", align_bytes=64) for h in range(HALVES)]
+        cols = HALF // 16
+
+        def gather_tokens(h):
+            part = list1[:, h * cols : (h + 1) * cols]
+            nc.vector.tensor_copy(g_plane[h][:], x_plane[:].indirect(part))
+            nc.vector.tensor_copy(g_words[h][:], x_words[:].indirect(part))
+
+        spread(s1_raw)
+        nc.scalar.copy(w2_dealt[:].rearrange("p (t m) -> p m t", t=PACK), w2_raw[:].rearrange("p (m t) -> p m t", t=PACK))
+        nc.scalar.copy(dealt(w_dealt[:]), natural(w_raw[:]))
+        nc.vector.tensor_copy(dealt(w2_plane[:]), natural(s1_raw[:, 0, 0:R]))
+        gather_tokens(0)
+        nc.vector.tensor_copy(dealt(w_plane[:]), natural(s1_raw[:, 0, R : 2 * R]))
+        gather_tokens(1)
+        spread(s2_raw)
+
+        h_words = sb.tile([P, J], U32, name="h_words", align_bytes=64)
+        h_plane = sb.tile([P, J], U8, name="h_plane", align_bytes=64)
+        q_sb = sb.tile([P, NT * J], F32, name="q_sb")
+        for h in range(HALVES):
+            b_ps = ps.tile([P, PACK, HALF], F32, name=f"b_ps{h}")
+            a_ps = ps.tile([P, PACK, HALF], F32, name=f"a_ps{h}")
+            for t in range(PACK):
+                nc.tensor.matmul_mx(
+                    out=b_ps[:, t, :],
+                    lhsT=w2_dealt[:, t * P : (t + 1) * P].bitcast(E4M3),
+                    lhsT_scale=w2_plane[:, t * P : (t + 1) * P],
+                    rhs=g_words[h][:].bitcast(E5M2), rhs_scale=g_plane[h][:], start=True, stop=True,
+                )
+            for t in range(PACK):
+                nc.tensor.matmul_mx(
+                    out=a_ps[:, t, :],
+                    lhsT=w_dealt[:, t * P : (t + 1) * P].bitcast(E2M1),
+                    lhsT_scale=w_plane[:, t * P : (t + 1) * P],
+                    rhs=g_words[h][:].bitcast(E5M2), rhs_scale=g_plane[h][:], start=True, stop=True,
+                )
+            b_sb = sb.tile([P, HALF, PACK], F32, name=f"b_sb{h}")
+            hid = sb.tile([P, HALF, PACK], BF16, name="hid", align_bytes=64)
+            nc.scalar.copy(b_sb[:], b_ps[:].rearrange("p t j -> p j t"))
+            nc.vector.tensor_tensor(hid[:], a_ps[:].rearrange("p t j -> p j t"), b_sb[:], ALU.max)
+            js = slice(h * HALF, (h + 1) * HALF)
+            nc.vector.quantize_mx(
+                out=h_words[:, js].bitcast(E4M3), scales=h_plane[:, js], in_=hid[:].rearrange("p j t -> p (j t)")
+            )
+        for h in range(HALVES):
+            js = slice(h * HALF, (h + 1) * HALF)
+            p_ps = ps.tile([P, NT, HALF], F32, name=f"p_ps{h}")
+            for i in range(NT):
+                nc.tensor.matmul_mx(
+                    out=p_ps[:, i, :],
+                    lhsT=wb_sb[:, 2 * i * P : 2 * (i + 1) * P].bitcast(E2M1),
+                    lhsT_scale=s2_plane[:, i * P : (i + 1) * P],
+                    rhs=h_words[:, js].bitcast(E4M3), rhs_scale=h_plane[:, js], start=True, stop=True,
+                )
+            q_ps = ps.tile([P, NT, HALF], F32, name=f"q_ps{h}")
+            for i in range(NT):
+                nc.tensor.matmul_mx(
+                    out=q_ps[:, i, :],
+                    lhsT=wc_sb[:, i * P : (i + 1) * P].bitcast(E4M3),
+                    lhsT_scale=s2_plane[:, N + i * P : N + (i + 1) * P],
+                    rhs=h_words[:, js].bitcast(E4M3), rhs_scale=h_plane[:, js], start=True, stop=True,
+                )
+            p_sb = sb.tile([P, NT, HALF], F32, name=f"p_sb{h}", tag=f"b_sb{1 - h}")
+            nc.scalar.copy(p_sb[:], p_ps[:])
+            nc.vector.tensor_copy(q_sb[:].rearrange("p (i j) -> p i j", i=NT)[:, :, js], q_ps[:])
+            part = list2[:, h * cols : (h + 1) * cols]
+            nc.vector.tensor_copy(boards[0][:].indirect(part), p_sb[:, 0, :])
+            nc.scalar.activation(boards[1][:].indirect(part), p_sb[:, 1, :], COPY)
+
+        q_pick = [sb.tile([P, O], F32, name="q_pick0", tag="b_sb0"), sb.tile([P, O], F32, name="q_pick1")]
+        pw_pick = sb.tile([P, NT, O], F32, name="pw_pick")
+        diff = sb.tile([P, NT, O], F32, name="diff")
+        res = sb.tile([P, NT, O], F32, name="res")
+        for i in (1, 0):
+            nc.vector.tensor_copy(q_pick[i][:], q_sb[:, i * J : (i + 1) * J].indirect(list4[:]))
+        for i in (1, 0):
+            nc.scalar.activation(pw_pick[:, i, :], boards[i][:].indirect(list3[:]), COPY, scale=so_sb[:, i : i + 1])
+        for i in (1, 0):
+            nc.vector.tensor_tensor(diff[:, i, :], pw_pick[:, i, :], q_pick[i][:], ALU.subtract)
+        for i in (1, 0):
+            nc.vector.scalar_tensor_tensor(res[:, i, :], diff[:, i, :], -1.0, diff[:, i, :], ALU.mult, ALU.max)
+            nc.sync.dma_start(out[i * P : (i + 1) * P, :], res[:, i, :])

@@ -21,8 +21,9 @@ P = 128
 PACK = 4
 QUADS = 4
 QUAD = 32
-HALF = J // 2
+UPPER = P // 2
 HALVES = 2
+HALF = J // HALVES
 NT = N // P
 
 
@@ -41,41 +42,49 @@ def tile_list_outcomeboard_twow_kernel(
         def flat_words(words):
             return words[0].rearrange("p c t -> p (c t)").bitcast(I32)
 
+        def spread(plane, stage):
+            for q in range(QUADS):
+                nc.vector.tensor_copy(plane[QUAD * q : QUAD * q + PACK, :].bitcast(I32), stage[:, q, :])
+
+        def dealt(ap):
+            return ap.rearrange("p (t m) -> p t m", t=PACK)
+
+        def natural(ap):
+            return ap.rearrange("p (m t) -> p t m", t=PACK)
+
         list1 = sb.tile([P, J // 16], U16, name="list1")
         list2 = sb.tile([P, J // 16], U16, name="list2")
         list3 = sb.tile([P, O // 16], U16, name="list3")
         list4 = sb.tile([P, O // 16], U16, name="list4")
         x_words = sb.tile([P, T], U32, name="x_words", align_bytes=64)
+        x_stage = sb.tile([P, 2, T // 4], I32, name="x_stage")
         x_plane = sb.tile([P, T], U8, name="x_plane", align_bytes=64)
-        w2_raw = sb.tile([P, R], U32, name="w2_raw", align_bytes=64)
-        w_raw = sb.tile([P, R], U16, name="w_raw", align_bytes=64)
-        s1_raw = sb.tile([P, QUADS, 2 * R], U8, name="s1_raw", align_bytes=64)
-        w2_plane = sb.tile([P, R], U8, name="w2_plane", align_bytes=64)
-        w_plane = sb.tile([P, R], U8, name="w_plane", align_bytes=64)
-        w2_dealt = sb.tile([P, R], U32, name="w2_dealt", align_bytes=64)
+        w_raw = sb.tile([P, R], U16, name="w_raw")
+        w2_raw = sb.tile([P, R], U32, name="w2_raw")
+        s1_stage = sb.tile([PACK, QUADS, 2 * R // 4], I32, name="s1_stage")
+        s1_raw = sb.tile([P, 2 * R], U8, name="s1_raw", align_bytes=64)
         w_dealt = sb.tile([P, R], U16, name="w_dealt", align_bytes=64)
+        w2_dealt = sb.tile([P, R], U32, name="w2_dealt", align_bytes=64)
+        w_plane = sb.tile([P, R], U8, name="w_plane", align_bytes=64)
         wb_sb = sb.tile([P, 2 * N], U8, name="wb_sb", align_bytes=64)
         wc_sb = sb.tile([P, N], U32, name="wc_sb", align_bytes=64)
-        s2_raw = sb.tile([P, QUADS, 2 * N], U8, name="s2_raw", align_bytes=64)
-        s2_plane = s2_raw[:, 0, :]
+        s2_stage = sb.tile([PACK, QUADS, 2 * N // 4], I32, name="s2_stage")
         so_sb = sb.tile([P, NT], F32, name="so_sb")
         boards = [sb.tile([P, C], F32, name=f"board{i}") for i in range(NT)]
 
-        nc.vector.memset(s1_raw[:, 0, :].bitcast(I32), 0)
-        nc.vector.memset(x_plane[:].bitcast(I32), 0)
-        nc.vector.memset(s2_plane.bitcast(I32), 0)
-        nc.scalar.dma_start(x_words[:].bitcast(I32), flat_words(xt_words))
-        nc.gpsimd.dma_start(w2_raw[:].bitcast(I32), flat_words(w2_words))
-        nc.gpsimd.dma_start(w_raw[:].bitcast(I32), w_words[0].bitcast(I32))
+        nc.vector.memset(x_stage[UPPER:P, :, :], 0)
+        nc.vector.memset(s1_raw[:].bitcast(I32), 0)
+        nc.sync.dma_start(s1_stage[:, :, 0 : R // 4], staged_rows(w_scales))
+        nc.sync.dma_start(s1_stage[:, :, R // 4 : 2 * R // 4], staged_rows(w2_scales))
         nc.sync.dma_start(list1[:], offs)
-        nc.sync.dma_start(s1_raw[0:PACK, :, 0:R].bitcast(I32), staged_rows(w2_scales))
-        nc.sync.dma_start(s1_raw[0:PACK, :, R : 2 * R].bitcast(I32), staged_rows(w_scales))
-        for q in range(QUADS):
-            nc.sync.dma_start(
-                x_plane[QUAD * q : QUAD * q + PACK, :].bitcast(I32), xt_scales[0, PACK * q : PACK * (q + 1), :].bitcast(I32)
-            )
-        nc.sync.dma_start(s2_raw[0:PACK, :, 0:N].bitcast(I32), staged_rows(wb_scales))
-        nc.sync.dma_start(s2_raw[0:PACK, :, N : 2 * N].bitcast(I32), staged_rows(wc_scales))
+        nc.sync.dma_start(w_raw[:].bitcast(I32), w_words[0].bitcast(I32))
+        x_rows = xt_scales[0].bitcast(I32).rearrange("(u q r) c -> q r u c", u=2, r=PACK)
+        for q in range(2):
+            nc.sync.dma_start(x_stage[UPPER + QUAD * q : UPPER + QUAD * q + PACK, :, :], x_rows[q])
+        nc.sync.dma_start(x_words[:].bitcast(I32), flat_words(xt_words))
+        nc.sync.dma_start(w2_raw[:].bitcast(I32), flat_words(w2_words))
+        nc.sync.dma_start(s2_stage[:, :, 0 : N // 4], staged_rows(wb_scales))
+        nc.sync.dma_start(s2_stage[:, :, N // 4 : 2 * N // 4], staged_rows(wc_scales))
         nc.sync.dma_start(wb_sb[:].bitcast(I32), wb_words[0].bitcast(I32))
         nc.sync.dma_start(wc_sb[:].bitcast(I32), flat_words(wc_words))
         nc.sync.dma_start(list2[:], offs2)
@@ -86,97 +95,94 @@ def tile_list_outcomeboard_twow_kernel(
         for board in boards:
             nc.vector.memset(board[:], 0.0)
 
-        def spread(raw):
-            for q in range(1, QUADS):
-                nc.vector.tensor_copy(raw[QUAD * q : QUAD * q + PACK, 0, :].bitcast(I32), raw[0:PACK, q, :].bitcast(I32))
-
-        def dealt(ap):
-            return ap.rearrange("p (t m) -> p t m", t=PACK)
-
-        def natural(ap):
-            return ap.rearrange("p (m t) -> p t m", t=PACK)
-
-        g_words = [sb.tile([P, HALF], U32, name=f"g_words{h}", align_bytes=64) for h in range(HALVES)]
-        g_plane = [sb.tile([P, HALF], U8, name=f"g_plane{h}", align_bytes=64) for h in range(HALVES)]
-        cols = HALF // 16
-
-        def gather_tokens(h):
-            part = list1[:, h * cols : (h + 1) * cols]
-            nc.vector.tensor_copy(g_plane[h][:], x_plane[:].indirect(part))
-            nc.vector.tensor_copy(g_words[h][:], x_words[:].indirect(part))
-
-        spread(s1_raw)
-        nc.scalar.copy(w2_dealt[:].rearrange("p (t m) -> p m t", t=PACK), w2_raw[:].rearrange("p (m t) -> p m t", t=PACK))
+        spread(s1_raw, s1_stage)
         nc.scalar.copy(dealt(w_dealt[:]), natural(w_raw[:]))
-        nc.vector.tensor_copy(dealt(w2_plane[:]), natural(s1_raw[:, 0, 0:R]))
-        gather_tokens(0)
-        nc.vector.tensor_copy(dealt(w_plane[:]), natural(s1_raw[:, 0, R : 2 * R]))
-        gather_tokens(1)
-        spread(s2_raw)
+        nc.scalar.copy(w2_dealt[:].rearrange("p (t m) -> p m t", t=PACK), w2_raw[:].rearrange("p (m t) -> p m t", t=PACK))
+        for u in range(2):
+            nc.vector.tensor_copy(x_plane[UPPER * u : UPPER * (u + 1), :].bitcast(I32), x_stage[UPPER:P, u, :])
+        nc.vector.tensor_copy(dealt(w_plane[:]), natural(s1_raw[:, 0:R]))
 
+        g_plane = sb.tile([P, J], U8, name="g_plane", align_bytes=64)
+        g_words = [sb.tile([P, HALF], U32, name=f"g_words{h}", align_bytes=64) for h in range(HALVES)]
+        cols = HALF // 16
+        nc.vector.tensor_copy(g_plane[:], x_plane[:].indirect(list1[:]))
+        for h in range(HALVES):
+            nc.vector.tensor_copy(g_words[h][:], x_words[:].indirect(list1[:, h * cols : (h + 1) * cols]))
+
+        w2_plane = sb.tile([P, R], U8, name="w2_plane", tag="x_words", align_bytes=64)
+        nc.vector.tensor_copy(dealt(w2_plane[:]), natural(s1_raw[:, R : 2 * R]))
+        s2_plane = sb.tile([P, 2 * N], U8, name="s2_plane", tag="s1_raw", align_bytes=64)
+        nc.vector.memset(s2_plane[:].bitcast(I32), 0)
+        spread(s2_plane, s2_stage)
+
+        halves = [slice(h * HALF, (h + 1) * HALF) for h in range(HALVES)]
+        a_ps = [ps.tile([P, PACK, HALF], F32, name=f"a_ps{h}") for h in range(HALVES)]
+        b_ps = [ps.tile([P, PACK, HALF], F32, name=f"b_ps{h}") for h in range(HALVES)]
+        for banks, words, plane, fmt in ((a_ps, w_dealt, w_plane, E2M1), (b_ps, w2_dealt, w2_plane, E4M3)):
+            for h in range(HALVES):
+                for t in range(PACK):
+                    nc.tensor.matmul_mx(
+                        out=banks[h][:, t, :],
+                        lhsT=words[:, t * P : (t + 1) * P].bitcast(fmt),
+                        lhsT_scale=plane[:, t * P : (t + 1) * P],
+                        rhs=g_words[h][:].bitcast(E5M2), rhs_scale=g_plane[:, halves[h]], start=True, stop=True,
+                    )
+        a_sb = [sb.tile([P, HALF, PACK], F32, name=f"a_sb{h}") for h in range(HALVES)]
+        hid = [sb.tile([P, HALF, PACK], BF16, name=f"hid{h}", align_bytes=64) for h in range(HALVES)]
         h_words = sb.tile([P, J], U32, name="h_words", align_bytes=64)
         h_plane = sb.tile([P, J], U8, name="h_plane", align_bytes=64)
-        q_sb = sb.tile([P, NT * J], F32, name="q_sb")
         for h in range(HALVES):
-            b_ps = ps.tile([P, PACK, HALF], F32, name=f"b_ps{h}")
-            a_ps = ps.tile([P, PACK, HALF], F32, name=f"a_ps{h}")
-            for t in range(PACK):
-                nc.tensor.matmul_mx(
-                    out=b_ps[:, t, :],
-                    lhsT=w2_dealt[:, t * P : (t + 1) * P].bitcast(E4M3),
-                    lhsT_scale=w2_plane[:, t * P : (t + 1) * P],
-                    rhs=g_words[h][:].bitcast(E5M2), rhs_scale=g_plane[h][:], start=True, stop=True,
-                )
-            for t in range(PACK):
-                nc.tensor.matmul_mx(
-                    out=a_ps[:, t, :],
-                    lhsT=w_dealt[:, t * P : (t + 1) * P].bitcast(E2M1),
-                    lhsT_scale=w_plane[:, t * P : (t + 1) * P],
-                    rhs=g_words[h][:].bitcast(E5M2), rhs_scale=g_plane[h][:], start=True, stop=True,
-                )
-            b_sb = sb.tile([P, HALF, PACK], F32, name=f"b_sb{h}")
-            hid = sb.tile([P, HALF, PACK], BF16, name="hid", align_bytes=64)
-            nc.scalar.copy(b_sb[:], b_ps[:].rearrange("p t j -> p j t"))
-            nc.vector.tensor_tensor(hid[:], a_ps[:].rearrange("p t j -> p j t"), b_sb[:], ALU.max)
-            js = slice(h * HALF, (h + 1) * HALF)
+            nc.scalar.copy(a_sb[h][:], a_ps[h][:].rearrange("p t j -> p j t"))
+        for h in range(HALVES):
+            nc.vector.tensor_tensor(hid[h][:], b_ps[h][:].rearrange("p t j -> p j t"), a_sb[h][:], ALU.max)
+        for h in range(HALVES):
             nc.vector.quantize_mx(
-                out=h_words[:, js].bitcast(E4M3), scales=h_plane[:, js], in_=hid[:].rearrange("p j t -> p (j t)")
+                out=h_words[:, halves[h]].bitcast(E4M3), scales=h_plane[:, halves[h]],
+                in_=hid[h][:].rearrange("p j t -> p (j t)"),
             )
+
+        p_ps = [ps.tile([P, NT, HALF], F32, name=f"p_ps{h}") for h in range(HALVES)]
+        q_ps = [ps.tile([P, J], F32, name=f"q_ps{i}") for i in range(NT)]
         for h in range(HALVES):
-            js = slice(h * HALF, (h + 1) * HALF)
-            p_ps = ps.tile([P, NT, HALF], F32, name=f"p_ps{h}")
             for i in range(NT):
                 nc.tensor.matmul_mx(
-                    out=p_ps[:, i, :],
+                    out=p_ps[h][:, i, :],
                     lhsT=wb_sb[:, 2 * i * P : 2 * (i + 1) * P].bitcast(E2M1),
                     lhsT_scale=s2_plane[:, i * P : (i + 1) * P],
-                    rhs=h_words[:, js].bitcast(E4M3), rhs_scale=h_plane[:, js], start=True, stop=True,
+                    rhs=h_words[:, halves[h]].bitcast(E4M3), rhs_scale=h_plane[:, halves[h]], start=True, stop=True,
                 )
-            q_ps = ps.tile([P, NT, HALF], F32, name=f"q_ps{h}")
-            for i in range(NT):
-                nc.tensor.matmul_mx(
-                    out=q_ps[:, i, :],
-                    lhsT=wc_sb[:, i * P : (i + 1) * P].bitcast(E4M3),
-                    lhsT_scale=s2_plane[:, N + i * P : N + (i + 1) * P],
-                    rhs=h_words[:, js].bitcast(E4M3), rhs_scale=h_plane[:, js], start=True, stop=True,
-                )
-            p_sb = sb.tile([P, NT, HALF], F32, name=f"p_sb{h}", tag=f"b_sb{1 - h}")
-            nc.scalar.copy(p_sb[:], p_ps[:])
-            nc.vector.tensor_copy(q_sb[:].rearrange("p (i j) -> p i j", i=NT)[:, :, js], q_ps[:])
-            part = list2[:, h * cols : (h + 1) * cols]
-            nc.vector.tensor_copy(boards[0][:].indirect(part), p_sb[:, 0, :])
-            nc.scalar.activation(boards[1][:].indirect(part), p_sb[:, 1, :], COPY)
+        for i in range(NT):
+            nc.tensor.matmul_mx(
+                out=q_ps[i][:],
+                lhsT=wc_sb[:, i * P : (i + 1) * P].bitcast(E4M3),
+                lhsT_scale=s2_plane[:, N + i * P : N + (i + 1) * P],
+                rhs=h_words[:].bitcast(E4M3), rhs_scale=h_plane[:], start=True, stop=True,
+            )
+        p_sb = [sb.tile([P, NT, HALF], F32, name=f"p_sb{h}") for h in range(HALVES)]
+        q_sb = [sb.tile([P, J], F32, name=f"q_sb{i}") for i in range(NT)]
+        nc.scalar.copy(p_sb[0][:], p_ps[0][:])
+        nc.vector.tensor_copy(p_sb[1][:], p_ps[1][:])
 
-        q_pick = [sb.tile([P, O], F32, name="q_pick0", tag="b_sb0"), sb.tile([P, O], F32, name="q_pick1")]
+        def put(h):
+            part = list2[:, h * cols : (h + 1) * cols]
+            nc.vector.tensor_copy(boards[0][:].indirect(part), p_sb[h][:, 0, :])
+            nc.scalar.activation(boards[1][:].indirect(part), p_sb[h][:, 1, :], COPY)
+
+        put(0)
+        nc.vector.tensor_copy(q_sb[0][:], q_ps[0][:])
+        nc.scalar.copy(q_sb[1][:], q_ps[1][:])
+        put(1)
+
+        q_pick = sb.tile([P, NT, O], F32, name="q_pick", tag="p_sb1")
         pw_pick = sb.tile([P, NT, O], F32, name="pw_pick")
         diff = sb.tile([P, NT, O], F32, name="diff")
         res = sb.tile([P, NT, O], F32, name="res")
-        for i in (1, 0):
-            nc.vector.tensor_copy(q_pick[i][:], q_sb[:, i * J : (i + 1) * J].indirect(list4[:]))
-        for i in (1, 0):
+        for i in range(NT):
+            nc.vector.tensor_copy(q_pick[:, i, :], q_sb[i][:].indirect(list4[:]))
+        for i in range(NT):
             nc.scalar.activation(pw_pick[:, i, :], boards[i][:].indirect(list3[:]), COPY, scale=so_sb[:, i : i + 1])
-        for i in (1, 0):
-            nc.vector.tensor_tensor(diff[:, i, :], pw_pick[:, i, :], q_pick[i][:], ALU.subtract)
-        for i in (1, 0):
+        for i in range(NT):
+            nc.vector.tensor_tensor(diff[:, i, :], pw_pick[:, i, :], q_pick[:, i, :], ALU.subtract)
+        for i in range(NT):
             nc.vector.scalar_tensor_tensor(res[:, i, :], diff[:, i, :], -1.0, diff[:, i, :], ALU.mult, ALU.max)
             nc.sync.dma_start(out[i * P : (i + 1) * P, :], res[:, i, :])

from contextlib import ExitStack

import concourse.mybir as mybir

K, T, J, R, N, C, O = 512, 1024, 256, 512, 256, 512, 128
FLOPS = 2 * 2 * K * R * J + 2 * 2 * R * N * J

F32 = mybir.dt.float32
BF16 = mybir.dt.bfloat16
I32 = mybir.dt.int32
U32 = mybir.dt.uint32
U16 = mybir.dt.uint16
U8 = mybir.dt.uint8
E4M3 = mybir.dt.float8_e4m3fn_x4
E5M2 = mybir.dt.float8_e5m2_x4
E2M1 = mybir.dt.float4_e2m1fn_x4
ALU = mybir.AluOpType
COPY = mybir.ActivationFunctionType.Copy

P = 128
PACK = 4
QUADS = 4
QUAD = 32
UPPER = P // 2
HALVES = 2
HALF = J // HALVES
NT = N // P


def tile_list_outcomeboard_twow_kernel(
    tc, xt_words, xt_scales, w_words, w_scales, w2_words, w2_scales, wb_words, wb_scales,
    wc_words, wc_scales, so, offs, offs2, offs3, offs4, out,
):
    nc = tc.nc
    with ExitStack() as ctx:
        sb = ctx.enter_context(tc.tile_pool(name="sb", bufs=1))
        ps = ctx.enter_context(tc.psum_pool(name="ps", bufs=1))

        def staged_rows(scales):
            return scales[0].bitcast(I32).rearrange("(q r) c -> r q c", r=PACK)

        def flat_words(words):
            return words[0].rearrange("p c t -> p (c t)").bitcast(I32)

        def spread(plane, stage):
            for q in range(QUADS):
                nc.vector.tensor_copy(plane[QUAD * q : QUAD * q + PACK, :].bitcast(I32), stage[:, q, :])

        def dealt(ap):
            return ap.rearrange("p (t m) -> p t m", t=PACK)

        def natural(ap):
            return ap.rearrange("p (m t) -> p t m", t=PACK)

        list1 = sb.tile([P, J // 16], U16, name="list1")
        list2 = sb.tile([P, J // 16], U16, name="list2")
        list3 = sb.tile([P, O // 16], U16, name="list3")
        list4 = sb.tile([P, O // 16], U16, name="list4")
        x_words = sb.tile([P, T], U32, name="x_words", align_bytes=64)
        x_stage = sb.tile([P, 2, T // 4], I32, name="x_stage")
        x_plane = sb.tile([P, T], U8, name="x_plane", align_bytes=64)
        w_raw = sb.tile([P, R], U16, name="w_raw")
        w2_raw = sb.tile([P, R], U32, name="w2_raw")
        s1_stage = sb.tile([PACK, QUADS, 2 * R // 4], I32, name="s1_stage")
        s1_raw = sb.tile([P, 2 * R], U8, name="s1_raw", align_bytes=64)
        w_dealt = sb.tile([P, R], U16, name="w_dealt", align_bytes=64)
        w2_dealt = sb.tile([P, R], U32, name="w2_dealt", align_bytes=64)
        w_plane = sb.tile([P, R], U8, name="w_plane", align_bytes=64)
        wb_sb = sb.tile([P, 2 * N], U8, name="wb_sb", align_bytes=64)
        wc_sb = sb.tile([P, N], U32, name="wc_sb", align_bytes=64)
        s2_stage = sb.tile([PACK, QUADS, 2 * N // 4], I32, name="s2_stage")
        so_sb = sb.tile([P, NT], F32, name="so_sb")
        boards = [sb.tile([P, C], F32, name=f"board{i}") for i in range(NT)]

        nc.vector.memset(x_stage[UPPER:P, :, :], 0)
        nc.vector.memset(s1_raw[:].bitcast(I32), 0)
        nc.sync.dma_start(s1_stage[:, :, 0 : R // 4], staged_rows(w_scales))
        nc.sync.dma_start(s1_stage[:, :, R // 4 : 2 * R // 4], staged_rows(w2_scales))
        nc.sync.dma_start(list1[:], offs)
        nc.sync.dma_start(w_raw[:].bitcast(I32), w_words[0].bitcast(I32))
        x_rows = xt_scales[0].bitcast(I32).rearrange("(u q r) c -> q r u c", u=2, r=PACK)
        for q in range(2):
            nc.sync.dma_start(x_stage[UPPER + QUAD * q : UPPER + QUAD * q + PACK, :, :], x_rows[q])
        nc.sync.dma_start(x_words[:].bitcast(I32), flat_words(xt_words))
        nc.sync.dma_start(w2_raw[:].bitcast(I32), flat_words(w2_words))
        nc.sync.dma_start(s2_stage[:, :, 0 : N // 4], staged_rows(wb_scales))
        nc.sync.dma_start(s2_stage[:, :, N // 4 : 2 * N // 4], staged_rows(wc_scales))
        nc.sync.dma_start(wb_sb[:].bitcast(I32), wb_words[0].bitcast(I32))
        nc.sync.dma_start(wc_sb[:].bitcast(I32), flat_words(wc_words))
        nc.sync.dma_start(list2[:], offs2)
        nc.sync.dma_start(list4[:], offs4)
        nc.sync.dma_start(list3[:], offs3)
        with nc.allow_non_contiguous_dma(reason="one weight a partition"):
            nc.sync.dma_start(so_sb[:], so.rearrange("(i p) one -> p (i one)", p=P))
        for board in boards:
            nc.vector.memset(board[:], 0.0)

        spread(s1_raw, s1_stage)
        nc.scalar.copy(dealt(w_dealt[:]), natural(w_raw[:]))
        nc.scalar.copy(w2_dealt[:].rearrange("p (t m) -> p m t", t=PACK), w2_raw[:].rearrange("p (m t) -> p m t", t=PACK))
        for u in range(2):
            nc.vector.tensor_copy(x_plane[UPPER * u : UPPER * (u + 1), :].bitcast(I32), x_stage[UPPER:P, u, :])
        nc.vector.tensor_copy(dealt(w_plane[:]), natural(s1_raw[:, 0:R]))

        g_plane = sb.tile([P, J], U8, name="g_plane", align_bytes=64)
        g_words = [sb.tile([P, HALF], U32, name=f"g_words{h}", align_bytes=64) for h in range(HALVES)]
        cols = HALF // 16
        nc.vector.tensor_copy(g_plane[:], x_plane[:].indirect(list1[:]))
        for h in range(HALVES):
            nc.vector.tensor_copy(g_words[h][:], x_words[:].indirect(list1[:, h * cols : (h + 1) * cols]))

        w2_plane = sb.tile([P, R], U8, name="w2_plane", tag="x_words", align_bytes=64)
        nc.vector.tensor_copy(dealt(w2_plane[:]), natural(s1_raw[:, R : 2 * R]))
        s2_plane = sb.tile([P, 2 * N], U8, name="s2_plane", tag="s1_raw", align_bytes=64)
        nc.vector.memset(s2_plane[:].bitcast(I32), 0)
        spread(s2_plane, s2_stage)

        halves = [slice(h * HALF, (h + 1) * HALF) for h in range(HALVES)]
        a_ps = [ps.tile([P, PACK, HALF], F32, name=f"a_ps{h}") for h in range(HALVES)]
        b_ps = [ps.tile([P, PACK, HALF], F32, name=f"b_ps{h}") for h in range(HALVES)]
        for banks, words, plane, fmt in ((a_ps, w_dealt, w_plane, E2M1), (b_ps, w2_dealt, w2_plane, E4M3)):
            for h in range(HALVES):
                for t in range(PACK):
                    nc.tensor.matmul_mx(
                        out=banks[h][:, t, :],
                        lhsT=words[:, t * P : (t + 1) * P].bitcast(fmt),
                        lhsT_scale=plane[:, t * P : (t + 1) * P],
                        rhs=g_words[h][:].bitcast(E5M2), rhs_scale=g_plane[:, halves[h]], start=True, stop=True,
                    )
        a_sb = [sb.tile([P, HALF, PACK], F32, name=f"a_sb{h}") for h in range(HALVES)]
        hid = [sb.tile([P, HALF, PACK], BF16, name=f"hid{h}", align_bytes=64) for h in range(HALVES)]
        h_words = sb.tile([P, J], U32, name="h_words", align_bytes=64)
        h_plane = sb.tile([P, J], U8, name="h_plane", align_bytes=64)
        for h in range(HALVES):
            nc.scalar.copy(a_sb[h][:], a_ps[h][:].rearrange("p t j -> p j t"))
        for h in range(HALVES):
            nc.vector.tensor_tensor(hid[h][:], b_ps[h][:].rearrange("p t j -> p j t"), a_sb[h][:], ALU.max)
        for h in range(HALVES):
            nc.vector.quantize_mx(
                out=h_words[:, halves[h]].bitcast(E4M3), scales=h_plane[:, halves[h]],
                in_=hid[h][:].rearrange("p j t -> p (j t)"),
            )

        p_ps = [ps.tile([P, NT, HALF], F32, name=f"p_ps{h}") for h in range(HALVES)]
        q_ps = [ps.tile([P, J], F32, name=f"q_ps{i}") for i in range(NT)]
        for h in range(HALVES):
            for i in range(NT):
                nc.tensor.matmul_mx(
                    out=p_ps[h][:, i, :],
                    lhsT=wb_sb[:, 2 * i * P : 2 * (i + 1) * P].bitcast(E2M1),
                    lhsT_scale=s2_plane[:, i * P : (i + 1) * P],
                    rhs=h_words[:, halves[h]].bitcast(E4M3), rhs_scale=h_plane[:, halves[h]], start=True, stop=True,
                )
        for i in range(NT):
            nc.tensor.matmul_mx(
                out=q_ps[i][:],
                lhsT=wc_sb[:, i * P : (i + 1) * P].bitcast(E4M3),
                lhsT_scale=s2_plane[:, N + i * P : N + (i + 1) * P],
                rhs=h_words[:].bitcast(E4M3), rhs_scale=h_plane[:], start=True, stop=True,
            )
        p_sb = [sb.tile([P, NT, HALF], F32, name=f"p_sb{h}") for h in range(HALVES)]
        q_sb = [sb.tile([P, J], F32, name=f"q_sb{i}") for i in range(NT)]
        nc.scalar.copy(p_sb[0][:], p_ps[0][:])
        nc.vector.tensor_copy(p_sb[1][:], p_ps[1][:])

        def put(h):
            part = list2[:, h * cols : (h + 1) * cols]
            nc.vector.tensor_copy(boards[0][:].indirect(part), p_sb[h][:, 0, :])
            nc.scalar.activation(boards[1][:].indirect(part), p_sb[h][:, 1, :], COPY)

        put(0)
        nc.vector.tensor_copy(q_sb[0][:], q_ps[0][:])
        nc.scalar.copy(q_sb[1][:], q_ps[1][:])
        put(1)

        q_pick = sb.tile([P, NT, O], F32, name="q_pick", tag="p_sb1")
        pw_pick = sb.tile([P, NT, O], F32, name="pw_pick")
        diff = sb.tile([P, NT, O], F32, name="diff")
        res = sb.tile([P, NT, O], F32, name="res")
        for i in range(NT):
            nc.vector.tensor_copy(q_pick[:, i, :], q_sb[i][:].indirect(list4[:]))
        for i in range(NT):
            nc.scalar.activation(pw_pick[:, i, :], boards[i][:].indirect(list3[:]), COPY, scale=so_sb[:, i : i + 1])
        for i in range(NT):
            nc.vector.tensor_tensor(diff[:, i, :], pw_pick[:, i, :], q_pick[:, i, :], ALU.subtract)
        for i in range(NT):
            nc.vector.scalar_tensor_tensor(res[:, i, :], diff[:, i, :], -1.0, diff[:, i, :], ALU.mult, ALU.max)
            nc.sync.dma_start(out[i * P : (i + 1) * P, :], res[:, i, :])
